import numpy as np, ml_dtypes
CORES = [35,38,43,46]
N = 4
import mx_ref
BF = ml_dtypes.bfloat16
def entries(a):
    return np.ascontiguousarray(a.T).reshape(-1)
def table(e):
    return np.ascontiguousarray(np.reshape(e, (-1, 16)).T).astype(np.int32)
def cols(t, e):
    v = np.concatenate([t.reshape(128, -1, 4), np.zeros((128, 1, 4), BF)], axis=1)
    return np.ascontiguousarray(v[:, e]).reshape(128, -1)
def tile(rs):
    return np.stack(rs, axis=2).reshape(128, -1).astype(BF)
def f(rng, *shape):
    return mx_ref.flush((rng.standard_normal(shape, dtype=np.float32) * np.exp2(rng.integers(-2, 3, shape[:-1] + (1,)))).astype(BF))
def wide(rng, *shape, cols=0):
    v = rng.standard_normal(shape, dtype=np.float32) * np.exp2(rng.integers(-12, 13, shape)).astype(np.float32)
    if cols: v *= np.repeat(np.exp2(rng.integers(-cols, cols + 1, shape[:-2] + (1, shape[-1] // 4))) * (rng.random(shape[:-2] + (1, shape[-1] // 4)) > 0.0625), 4, axis=-1).astype(np.float32)
    return mx_ref.flush(v.astype(BF))
T, E, EC, CAPP = 384, 4, 128, 112
def lists(rng, case=""):
    sn, so = np.full((N, N, CAPP), -1), np.full((N, E, EC), -1)
    lone = rng.integers(0, N)
    for d in range(N):
        a = rng.integers(0, E)
        n = rng.integers(CAPP // 4, CAPP + 1, N)
        if case == "full": n[:] = CAPP
        if case == "empty": n[(d + 1) % N] = 0
        if case == "empty" and d == lone: n[np.arange(N) != d] = 0
        used = np.concatenate([s * CAPP + (np.arange(n[s]) if case == "sorted" else rng.permutation(CAPP)[:n[s]]) for s in range(N)])
        if case == "one": used = rng.permutation(N * CAPP)[:EC + rng.integers(E - 1, 8 * E - 7)]
        if case != "sorted": used = rng.permutation(used)
        if case == "empty": used = used[:(E - 1) * EC]
        key = rng.random((E, EC)) * np.exp2(rng.integers(-1, 2, (E, 1)))
        if case in ("full", "one"): key[a] = -1
        if case == "empty": key[a] = 9
        who = np.argsort(key.reshape(-1))[:len(used)] // EC
        if case == "sorted": who = np.sort(who)
        for m in range(E):
            k = used[who == m]; so[d, m, :len(k)] = k
        sn[used // CAPP, d, used % CAPP] = rng.integers(0, T, len(used))
        if case == "sorted":
            for s in range(N): sn[s, d, :n[s]] = np.sort(sn[s, d, :n[s]])
    return {"sn": np.stack([table(q) for q in sn]), "so": np.stack([table(q) for q in so])}
def setup_inputs(rng):
    return {"x": f(rng, N, 128, 4 * T), "w": f(rng, N, 128, 2048 * E), "v": f(rng, N, 128, 512 * E), **lists(rng)}
def setup_inputs_full(rng):
    return {**setup_inputs(rng), **lists(rng, "full")}
def setup_inputs_one(rng):
    return {**setup_inputs(rng), **lists(rng, "one")}
def setup_inputs_empty(rng):
    return {**setup_inputs(rng), **lists(rng, "empty")}
def setup_inputs_sorted(rng):
    return {**setup_inputs(rng), **lists(rng, "sorted")}
def setup_inputs_spread(rng):
    d = setup_inputs(rng); d["x"] = wide(rng, N, 128, 4 * T, cols=6); return d
def check_inputs(d):
    b = []
    for r in range(N):
        c, e = entries(d["sn"][r]), entries(d["so"][r]).reshape(E, EC)
        if c.min() < -1 or c.max() >= T: b.append("sn")
        got = np.concatenate([entries(d["sn"][s])[r * CAPP:(r + 1) * CAPP] for s in range(N)])
        if e.min() < -1 or ((e[:, 1:] >= 0) & (e[:, :-1] < 0)).any() or np.sort(e[e >= 0]).tolist() != np.flatnonzero(got >= 0).tolist(): b.append("so")
    return b
def reference(x, w, v, sn, so):
    y = np.zeros((N, 128, E * EC), np.float32)
    for r in range(N):
        arrived = np.concatenate([cols(x[s], entries(sn[s])[r * CAPP:(r + 1) * CAPP]) for s in range(N)], axis=1)
        e = entries(so[r])
        for m in range(E):
            k = e[EC * m:EC * m + EC]
            t = mx_ref.quantize(cols(arrived, k))
            R = []
            for i in range(4):
                W = mx_ref.quantize(np.ascontiguousarray(w[r][:, 2048 * m + 512 * i:2048 * m + 512 * i + 512]))
                R.append(np.maximum(mx_ref.matmul(W, t), np.float32(0)) * np.float32(0.05))
            z = mx_ref.matmul(mx_ref.quantize(np.ascontiguousarray(v[r][:, 512 * m:512 * m + 512])), mx_ref.quantize(tile(R)))
            y[r][:, EC * m:EC * m + EC] = np.where(k >= 0, z, np.float32(0))
    return {"y": y}

@@ -1,0 +1,266 @@
+from concourse.bass import DstId, RemoteDMATransfer
+from concourse.mybir import AluOpType, ActivationFunctionType, dt
+
+CAPP, TOK, EXP, EC = 112, 384, 4, 128
+Z = 128
+LC = CAPP // 16
+F8 = "float8_e4m3fn_x4"
+
+LOADS = "x n w02 w23 ?aq w34 v04"
+SENDS = "aq as pq ps"
+VECTOR = "z n x a N p o w0 w1 l w2 P0 P1 P2 P3 R01 R03 w3 R11 Q0 R21 v04 R23 Q1 R31 Q2 R33 Q3 Y2 Y3"
+SCALAR = "a p o S0 S1 S2 S3 R00 R02 R10 R12 R13 R20 R22 R30 R32 Y0 Y1"
+TENSOR = "W0 W1 W2 W3 V0 V1 V2 V3"
+STORES = "02 23 34"
+PEER = 8
+
+SCRATCH = {
+    "xb": ("sbuf", [128, 4 * TOK], "bfloat16"),
+    "wb": ("sbuf", [128, 2048 * EXP], "bfloat16"),
+    "vb": ("sbuf", [128, 512 * EXP], "bfloat16"),
+    "zb": ("sbuf", [128, 4 * Z], "bfloat16"),
+    "sn32": ("sbuf", [128, 4 * LC], "int32"),
+    "so32": ("sbuf", [128, EXP * EC // 16], "int32"),
+    "snl": ("sbuf", [128, 64], "uint16"),
+    "sol": ("sbuf", [128, EXP * EC // 16], "uint16"),
+    "xq": ("sbuf", [128, TOK], F8), "xs": ("sbuf", [128, TOK], "uint8"),
+    "wq": ("sbuf", [128, 512 * EXP], F8), "ws": ("sbuf", [128, 512 * EXP], "uint8"),
+    "vq": ("sbuf", [128, 128 * EXP], F8), "vs": ("sbuf", [128, 128 * EXP], "uint8"),
+    "slotq": ("sbuf", [128, 4 * CAPP], F8), "slots": ("sbuf", [128, 4 * CAPP], "uint8"),
+    "landq": ("sbuf", [128, Z + 4 * CAPP], F8), "lands": ("sbuf", [128, Z + 4 * CAPP], "uint8"),
+    "tokq": ("sbuf", [128, EXP * EC], F8), "toks": ("sbuf", [128, EXP * EC], "uint8"),
+    "h": ("sbuf", [128, 4 * EXP * EC], "bfloat16"),
+    "hq": ("sbuf", [128, EXP * EC], F8), "hs": ("sbuf", [128, EXP * EC], "uint8"),
+    "yb": ("sbuf", [128, EXP * EC], "float32"),
+    "ps": ("psum", [128, 4096], "float32"),
+}
+SEMAPHORES = (["ldx", "ldsn", "ldso", "zfill", "zquant", "snA", "snB", "sol", "qx", "pqa", "pqp", "pqo", "psa", "psp", "pso",
+               "sentaq", "sentas", "sentpq", "sentps", "arrq", "arrs", "ydone"]
+              + [k + "%d" % m for k in ("ldw", "ldv", "qw", "qv", "tok", "qh", "vv", "yc") for m in range(EXP)]
+              + [k + "%d%d" % (m, b) for k in ("mm", "relu") for m in range(EXP) for b in range(4)])
+
+
+def routes(src, cores, topo):
+    away = [d for d, c in enumerate(cores) if topo.chip(c) != topo.chip(src)]
+    peer = [d for d, c in enumerate(cores) if topo.chip(c) == topo.chip(src) and c != src]
+    out, used = [], []
+    for i, d in enumerate(away):
+        es = topo.engines(src, cores[d])
+        k = len(es) // len(away)
+        out.append((d, es[i * k:(i + 1) * k]))
+        used += es[i * k:(i + 1) * k]
+    home = []
+    for d in peer:
+        es = [e for e in topo.engines(src, cores[d]) if e not in used]
+        home.append((d, es[::len(es) // PEER]))
+    return out, home
+
+
+def banks():
+    plan, held, i = {}, [None] * 8, 0
+    for t in TENSOR.split():
+        m = int(t[1])
+        for p in ([("W", m, b) for b in range(4)] if t[0] == "W" else [("V", m, 0)]):
+            k = i % 8
+            o = held[k]
+            plan[p] = (k, None if o is None else "relu%d%d" % o[1:] if o[0] == "W" else "yc%d" % o[1])
+            held[k] = p
+            i += 1
+    return plan
+
+
+def rank_program(g, core, T, topo):
+    rank = T.rank_of(core)
+    if rank is None:
+        return
+    S = T.sem
+    cores = list(T.cores)
+    ACT = ActivationFunctionType
+    away, home = routes(core, cores, topo)
+    first = away[0][0]
+    na = len(away)
+    peer = home[0][0]
+    arrive = sum(len(es) for c in cores if c != core
+                 for part in routes(c, cores, topo) for d, es in part if d == rank)
+    nsent = {"a": sum(len(es) for _, es in away), "p": sum(len(es) for _, es in home)}
+    tk = lambda s: s.split()
+
+    a = g.scalar
+    a.dma_start(T.sn32[0:16, :], T.sn[:]).then_inc(S.ldsn, 16)
+    for k in range(2):
+        a.dma_start(T.so32[16 * k:16 * k + 16, :], T.so[:]).then_inc(S.ldso, 16)
+
+    y = g.sync
+    ldof = {}
+    for s in tk(LOADS):
+        if s == "x":
+            y.dma_start(T.xb[:], T.x[:]).then_inc(S.ldx, 16)
+        elif s == "n":
+            y.dma_start(T.sn32[16:32, :], T.sn[:]).then_inc(S.ldsn, 16)
+        elif s[0] == "?":
+            y.wait_ge(S["sent" + s[1:]], nsent[s[1]])
+        else:
+            lo, hi = int(s[1]), int(s[2])
+            n, dst, src = (2048, T.wb, T.w) if s[0] == "w" else (512, T.vb, T.v)
+            for m in range(lo, hi):
+                ldof[s[0], m] = "ld%s%d" % (s[0], lo)
+            y.dma_start(dst[:, n * lo:n * hi], src[:, n * lo:n * hi]).then_inc(S["ld%s%d" % (s[0], lo)], 16)
+
+    def snoff(d, n):
+        c = d * LC
+        if c % 2:
+            c = 4 * LC + (d - 1) * LC
+        return T.snl[:, c:c + n * LC]
+
+    picks = {"a": ("slotq", "slots", 0, na * CAPP, snoff(first, na)),
+             "p": ("slotq", "slots", na * CAPP, (na + 1) * CAPP, snoff(peer, 1)),
+             "o": ("landq", "lands", Z + rank * CAPP, Z + (rank + 1) * CAPP, snoff(rank, 1))}
+
+    for s in tk(SENDS):
+        part, lo = (away, 0) if s[0] == "a" else (home, na)
+        trs = []
+        for i, (d, es) in enumerate(part):
+            rid, pid, _ = topo.addr(cores[d])
+            c0, l0 = (lo + i) * CAPP, Z + rank * CAPP
+            if s[1] == "q":
+                src, dst = T.slotq[:, c0:c0 + CAPP].bitcast(dt.uint8), T.landq[:, l0:l0 + CAPP].bitcast(dt.uint8)
+            else:
+                src, dst = T.slots[:, c0:c0 + CAPP], T.lands[:, l0:l0 + CAPP]
+            trs.append(RemoteDMATransfer(dst_ids=[DstId(rid=rid, pnc=pid)], dma_engine_mask=sum(1 << e for e in es),
+                                         remote_sem=S.arrq if s[1] == "q" else S.arrs, src=src, dst=dst))
+        g.wait_ge(S["p%s%s" % (s[1], s[0])], 1)
+        g.remote_dma_fused(trs, local_sem=S["sent" + s])
+    for s in tk(SENDS):
+        g.wait_ge(S["sent" + s], nsent[s[0]])
+
+    plan = banks()
+    v = g.vector
+    qvof = {}
+    for s in tk(VECTOR):
+        if s[0] == "v":
+            for m in range(int(s[1]), int(s[2])):
+                qvof[m] = "qv" + s[1]
+
+    def bank(p):
+        return T.ps[:, 512 * plan[p][0]:512 * plan[p][0] + EC]
+
+    def work(eng, order):
+        vec = eng is v
+        seen = []
+        for step in tk(order):
+            k = step[0]
+            if k == "z":
+                v.memset(T.zb[:], 0.0).then_inc(S.zfill, 1)
+                v.wait_ge(S.zfill, 1)
+                v.quantize_mx(T.landq[:, 0:Z], T.lands[:, 0:Z], T.zb[:]).then_inc(S.zquant, 1)
+                continue
+            if k == "n":
+                v.wait_ge(S.ldsn, 32)
+                for j in range(4):
+                    v.tensor_copy(T.snl[32 * j:32 * j + 32, 0:4 * LC], T.sn32[0:32, :]).then_inc(S.snA, 1)
+                continue
+            if k == "N":
+                for j in range(4):
+                    v.tensor_copy(T.snl[32 * j:32 * j + 32, 4 * LC:7 * LC], T.sn32[0:32, LC:4 * LC]).then_inc(S.snB, 1)
+                continue
+            if k == "l":
+                v.wait_ge(S.ldso, 32)
+                for j in range(4):
+                    v.tensor_scalar(T.sol[32 * j:32 * j + 32, :], T.so32[0:32, :], Z, None, AluOpType.add).then_inc(S.sol, 1)
+                continue
+            if k == "x":
+                v.wait_ge(S.ldx, 16)
+                v.quantize_mx(T.xq[:], T.xs[:], T.xb[:]).then_inc(S.qx, 1)
+                continue
+            if k in "apo":
+                if "x" not in seen:
+                    seen.append("x")
+                    eng.wait_ge(S.snA, 4)
+                    eng.wait_ge(S.qx, 1)
+                if k != "a" and "N" not in seen:
+                    seen.append("N")
+                    eng.wait_ge(S.snB, 4)
+                q, s, lo, hi, off = picks[k]
+                if vec:
+                    v.tensor_copy(T[q][:, lo:hi].bitcast(dt.uint32), T.xq[:, 0:TOK].bitcast(dt.uint32).indirect(off)).then_inc(S["pq" + k], 1)
+                else:
+                    a.activation(T[s][:, lo:hi], T.xs[:, 0:TOK].indirect(off), ACT.Copy).then_inc(S["ps" + k], 1)
+                continue
+            m = int(step[1])
+            lo, hi = EC * m, EC * m + EC
+            if k == "w":
+                eng.wait_ge(S[ldof["w", m]], 16)
+                v.quantize_mx(T.wq[:, 512 * m:512 * m + 512], T.ws[:, 512 * m:512 * m + 512],
+                              T.wb[:, 2048 * m:2048 * m + 2048]).then_inc(S["qw%d" % m], 1)
+            elif k == "v":
+                hi = EC * int(step[2])
+                for sm in sorted({ldof["v", j] for j in range(m, int(step[2]))}):
+                    eng.wait_ge(S[sm], 16)
+                v.quantize_mx(T.vq[:, lo:hi], T.vs[:, lo:hi], T.vb[:, 4 * lo:4 * hi]).then_inc(S["qv%d" % m], 1)
+            elif k in "PS":
+                if "w" not in seen:
+                    seen.append("w")
+                    eng.wait_ge(S.zquant, 1)
+                    eng.wait_ge(S.sol, 4)
+                    eng.wait_ge(S.pqo if vec else S.pso, 1)
+                    eng.wait_ge(S.arrq if vec else S.arrs, arrive)
+                off = T.sol[:, EC // 16 * m:EC // 16 * (m + 1)]
+                if vec:
+                    v.tensor_copy(T.tokq[:, lo:hi].bitcast(dt.uint32),
+                                  T.landq[:, 0:Z + 4 * CAPP].bitcast(dt.uint32).indirect(off)).then_inc(S["tok%d" % m], 1)
+                else:
+                    a.activation(T.toks[:, lo:hi], T.lands[:, 0:Z + 4 * CAPP].indirect(off), ACT.Copy).then_inc(S["tok%d" % m], 1)
+            elif k == "R":
+                b = int(step[2])
+                out, src, done = T.h[:, 4 * lo + b:4 * hi:4], bank(("W", m, b)), S["relu%d%d" % (m, b)]
+                eng.wait_ge(S["mm%d%d" % (m, b)], 1)
+                if vec:
+                    v.tensor_scalar(out, src, 0.0, 0.05, AluOpType.max, AluOpType.mult).then_inc(done, 1)
+                else:
+                    a.activation(out, src, ACT.Relu, scale=0.05).then_inc(done, 1)
+            elif k == "Q":
+                for b in range(4):
+                    eng.wait_ge(S["relu%d%d" % (m, b)], 1)
+                v.quantize_mx(T.hq[:, lo:hi], T.hs[:, lo:hi], T.h[:, 4 * lo:4 * hi]).then_inc(S["qh%d" % m], 1)
+            elif k == "Y":
+                eng.wait_ge(S["vv%d" % m], 1)
+                if vec:
+                    v.tensor_copy(T.yb[:, lo:hi], bank(("V", m, 0))).then_inc(S["yc%d" % m], 1)
+                else:
+                    a.activation(T.yb[:, lo:hi], bank(("V", m, 0)), ACT.Copy).then_inc(S["yc%d" % m], 1)
+
+    work(v, VECTOR)
+    work(a, SCALAR)
+
+    t = g.tensor
+    seen = []
+    for step in tk(TENSOR):
+        m = int(step[1])
+        lo, hi = EC * m, EC * m + EC
+        if step[0] == "W":
+            t.wait_ge(S["qw%d" % m], 1)
+            t.wait_ge(S["tok%d" % m], 2)
+            for b in range(4):
+                c = 512 * m + 128 * b
+                if plan[("W", m, b)][1]:
+                    t.wait_ge(S[plan[("W", m, b)][1]], 1)
+                t.matmul_mx(bank(("W", m, b)), T.wq[:, c:c + 128], T.ws[:, c:c + 128], T.tokq[:, lo:hi], T.toks[:, lo:hi],
+                            True, True).then_inc(S["mm%d%d" % (m, b)], 1)
+        else:
+            if qvof[m] not in seen:
+                seen.append(qvof[m])
+                t.wait_ge(S[qvof[m]], 1)
+            t.wait_ge(S["qh%d" % m], 1)
+            if plan[("V", m, 0)][1]:
+                t.wait_ge(S[plan[("V", m, 0)][1]], 1)
+            t.matmul_mx(bank(("V", m, 0)), T.vq[:, lo:lo + 128], T.vs[:, lo:lo + 128], T.hq[:, lo:hi], T.hs[:, lo:hi],
+                        True, True).then_inc(S["vv%d" % m], 1)
+
+    k = 0
+    for s in tk(STORES):
+        lo, hi = int(s[0]), int(s[1])
+        for m in range(lo, hi):
+            y.wait_ge(S["yc%d" % m], 1)
+        y.dma_start(T.y[:, EC * lo:EC * hi], T.yb[:, EC * lo:EC * hi]).then_inc(S.ydone, 16)
+        k += 16
+    y.wait_ge(S.ydone, k)

@@ -6,13 +6,18 @@ Z = 128
 LC = CAPP // 16
 F8 = "float8_e4m3fn_x4"
 
-LOADS = "x n w02 w23 ?aq w34 v04"
-SENDS = "aq as pq ps"
-VECTOR = "z n x a N p o w0 w1 l w2 P0 P1 P2 P3 R01 R03 w3 R11 Q0 R21 v04 R23 Q1 R31 Q2 R33 Q3 Y2 Y3"
-SCALAR = "a p o S0 S1 S2 S3 R00 R02 R10 R12 R13 R20 R22 R30 R32 Y0 Y1"
+SYNC = "n1 x0-2 x2-3 w0-8 w8-12 ? w12-16 v0-2 v2-4 y02 y23 y34"
+SENDS = "sAB qAB"
+VECTOR = ("z n x0-2 x2-3 As Aq Bq N oq l w0-4 w4-8 w8-12 P01 P12 P24 R03 w12-16 R13 Q0 v0-1 v1-2 R23 Q1 R31 R33 Q2 v2-3 v3-4 "
+          "Q3 Y3")
+SCALAR = "n0 l0 l1 Bs os S01 S12 S24 R00 R01 R02 R10 R11 R12 R20 R21 R22 R30 R32 Y0 Y1 Y2"
 TENSOR = "W0 W1 W2 W3 V0 V1 V2 V3"
-STORES = "02 23 34"
-PEER = 8
+PEER = 4
+
+
+def spans(order, kinds):
+    return [(s[0],) + tuple(int(n) for n in s[1:].split("-")) for s in order.split() if s[0] in kinds and "-" in s]
+
 
 SCRATCH = {
     "xb": ("sbuf", [128, 4 * TOK], "bfloat16"),
@@ -21,7 +26,7 @@ SCRATCH = {
     "zb": ("sbuf", [128, 4 * Z], "bfloat16"),
     "sn32": ("sbuf", [128, 4 * LC], "int32"),
     "so32": ("sbuf", [128, EXP * EC // 16], "int32"),
-    "snl": ("sbuf", [128, 64], "uint16"),
+    "snl": ("sbuf", [128, 40], "uint16"),
     "sol": ("sbuf", [128, EXP * EC // 16], "uint16"),
     "xq": ("sbuf", [128, TOK], F8), "xs": ("sbuf", [128, TOK], "uint8"),
     "wq": ("sbuf", [128, 512 * EXP], F8), "ws": ("sbuf", [128, 512 * EXP], "uint8"),
@@ -34,26 +39,28 @@ SCRATCH = {
     "yb": ("sbuf", [128, EXP * EC], "float32"),
     "ps": ("psum", [128, 4096], "float32"),
 }
-SEMAPHORES = (["ldx", "ldsn", "ldso", "zfill", "zquant", "snA", "snB", "sol", "qx", "pqa", "pqp", "pqo", "psa", "psp", "pso",
-               "sentaq", "sentas", "sentpq", "sentps", "arrq", "arrs", "ydone"]
-              + [k + "%d" % m for k in ("ldw", "ldv", "qw", "qv", "tok", "qh", "vv", "yc") for m in range(EXP)]
+SEMAPHORES = (["ldn", "ldl", "zfill", "zquant", "snA", "snB", "sol", "Aq", "As", "Bq", "Bs", "oq", "os",
+               "arrq", "arrs", "ydone", "issued"]
+              + ["sent%d" % i for i in range(len(SENDS.split()))]
+              + ["ld%s%d" % s[:2] for s in spans(SYNC + " " + SCALAR, "xwv")]
+              + ["q%s%d" % s[:2] for s in spans(VECTOR, "xwv")]
+              + [k + "%d" % m for k in ("P", "S", "qh", "vv", "yc") for m in range(EXP)]
               + [k + "%d%d" % (m, b) for k in ("mm", "relu") for m in range(EXP) for b in range(4)])
 
 
 def routes(src, cores, topo):
     away = [d for d, c in enumerate(cores) if topo.chip(c) != topo.chip(src)]
     peer = [d for d, c in enumerate(cores) if topo.chip(c) == topo.chip(src) and c != src]
-    out, used = [], []
+    out, used = {"A": [], "B": []}, []
     for i, d in enumerate(away):
         es = topo.engines(src, cores[d])
         k = len(es) // len(away)
-        out.append((d, es[i * k:(i + 1) * k]))
+        out["A"].append((d, es[i * k:(i + 1) * k]))
         used += es[i * k:(i + 1) * k]
-    home = []
     for d in peer:
         es = [e for e in topo.engines(src, cores[d]) if e not in used]
-        home.append((d, es[::len(es) // PEER]))
-    return out, home
+        out["B"].append((d, es[::len(es) // PEER]))
+    return out
 
 
 def banks():
@@ -75,192 +82,166 @@ def rank_program(g, core, T, topo):
         return
     S = T.sem
     cores = list(T.cores)
+    N = len(cores)
     ACT = ActivationFunctionType
-    away, home = routes(core, cores, topo)
-    first = away[0][0]
-    na = len(away)
-    peer = home[0][0]
+    dests = routes(core, cores, topo)
     arrive = sum(len(es) for c in cores if c != core
-                 for part in routes(c, cores, topo) for d, es in part if d == rank)
-    nsent = {"a": sum(len(es) for _, es in away), "p": sum(len(es) for _, es in home)}
-    tk = lambda s: s.split()
+                 for part in routes(c, cores, topo).values() for d, es in part if d == rank)
+    v, a, y, t = g.vector, g.scalar, g.sync, g.tensor
 
-    a = g.scalar
-    a.dma_start(T.sn32[0:16, :], T.sn[:]).then_inc(S.ldsn, 16)
-    for k in range(2):
-        a.dma_start(T.so32[16 * k:16 * k + 16, :], T.so[:]).then_inc(S.ldso, 16)
+    loaded = {(k, i): "ld%s%d" % (k, lo) for k, lo, hi in spans(SYNC + " " + SCALAR, "xwv") for i in range(lo, hi)}
+    packed = {(k, i): "q%s%d" % (k, lo) for k, lo, hi in spans(VECTOR, "xwv") for i in range(lo, hi)}
+    picked = {(s[0], m): s[:2] for s in (VECTOR + " " + SCALAR).split() if s[0] in "PS" for m in range(int(s[1]), int(s[2]))}
+    stores = [s for s in (SYNC + " " + SCALAR).split() if s[0] == "y"]
 
-    y = g.sync
-    ldof = {}
-    for s in tk(LOADS):
-        if s == "x":
-            y.dma_start(T.xb[:], T.x[:]).then_inc(S.ldx, 16)
-        elif s == "n":
-            y.dma_start(T.sn32[16:32, :], T.sn[:]).then_inc(S.ldsn, 16)
-        elif s[0] == "?":
-            y.wait_ge(S["sent" + s[1:]], nsent[s[1]])
-        else:
-            lo, hi = int(s[1]), int(s[2])
-            n, dst, src = (2048, T.wb, T.w) if s[0] == "w" else (512, T.vb, T.v)
-            for m in range(lo, hi):
-                ldof[s[0], m] = "ld%s%d" % (s[0], lo)
-            y.dma_start(dst[:, n * lo:n * hi], src[:, n * lo:n * hi]).then_inc(S["ld%s%d" % (s[0], lo)], 16)
+    shifted = rank * LC % 2 == 1
+    own = N * LC if shifted else rank * LC
+    picks = {"o": ("landq", "lands", Z + rank * CAPP, own, own + LC)}
+    for k in "AB":
+        c0, c1 = dests[k][0][0] * LC // 2 * 2, (dests[k][-1][0] + 1) * LC
+        picks[k] = ("slotq", "slots", 16 * c0, c0, c1)
 
-    def snoff(d, n):
-        c = d * LC
-        if c % 2:
-            c = 4 * LC + (d - 1) * LC
-        return T.snl[:, c:c + n * LC]
-
-    picks = {"a": ("slotq", "slots", 0, na * CAPP, snoff(first, na)),
-             "p": ("slotq", "slots", na * CAPP, (na + 1) * CAPP, snoff(peer, 1)),
-             "o": ("landq", "lands", Z + rank * CAPP, Z + (rank + 1) * CAPP, snoff(rank, 1))}
-
-    for s in tk(SENDS):
-        part, lo = (away, 0) if s[0] == "a" else (home, na)
+    nsent = []
+    for s in SENDS.split():
         trs = []
-        for i, (d, es) in enumerate(part):
-            rid, pid, _ = topo.addr(cores[d])
-            c0, l0 = (lo + i) * CAPP, Z + rank * CAPP
-            if s[1] == "q":
-                src, dst = T.slotq[:, c0:c0 + CAPP].bitcast(dt.uint8), T.landq[:, l0:l0 + CAPP].bitcast(dt.uint8)
-            else:
-                src, dst = T.slots[:, c0:c0 + CAPP], T.lands[:, l0:l0 + CAPP]
-            trs.append(RemoteDMATransfer(dst_ids=[DstId(rid=rid, pnc=pid)], dma_engine_mask=sum(1 << e for e in es),
-                                         remote_sem=S.arrq if s[1] == "q" else S.arrs, src=src, dst=dst))
-        g.wait_ge(S["p%s%s" % (s[1], s[0])], 1)
-        g.remote_dma_fused(trs, local_sem=S["sent" + s])
-    for s in tk(SENDS):
-        g.wait_ge(S["sent" + s], nsent[s[0]])
+        for k in s[1:]:
+            g.wait_ge(S[k + s[0]], 1)
+            for d, es in dests[k]:
+                rid, pid, _ = topo.addr(cores[d])
+                c0, l0 = d * CAPP, Z + rank * CAPP
+                if s[0] == "q":
+                    src, dst = T.slotq[:, c0:c0 + CAPP].bitcast(dt.uint8), T.landq[:, l0:l0 + CAPP].bitcast(dt.uint8)
+                else:
+                    src, dst = T.slots[:, c0:c0 + CAPP], T.lands[:, l0:l0 + CAPP]
+                trs.append(RemoteDMATransfer(dst_ids=[DstId(rid=rid, pnc=pid)], dma_engine_mask=sum(1 << e for e in es),
+                                             remote_sem=S["arr" + s[0]], src=src, dst=dst))
+        g.remote_dma_fused(trs, local_sem=S["sent%d" % len(nsent)])
+        nsent.append(sum(len(es) for k in s[1:] for _, es in dests[k]))
+    g.sem_inc(S.issued, 1)
+    for i, n in enumerate(nsent):
+        g.wait_ge(S["sent%d" % i], n)
 
     plan = banks()
-    v = g.vector
-    qvof = {}
-    for s in tk(VECTOR):
-        if s[0] == "v":
-            for m in range(int(s[1]), int(s[2])):
-                qvof[m] = "qv" + s[1]
 
     def bank(p):
         return T.ps[:, 512 * plan[p][0]:512 * plan[p][0] + EC]
 
     def work(eng, order):
-        vec = eng is v
         seen = []
-        for step in tk(order):
+
+        def wait(name, n=1):
+            if name and name not in seen:
+                seen.append(name)
+                eng.wait_ge(S[name], n)
+
+        def pick(out, win, off, done):
+            if eng is v:
+                v.tensor_copy(out, win.indirect(off)).then_inc(S[done], 1)
+            else:
+                a.activation(out, win.indirect(off), ACT.Copy).then_inc(S[done], 1)
+
+        for step in order.split():
             k = step[0]
-            if k == "z":
+            if k in "xwv":
+                lo, hi = (int(n) for n in step[1:].split("-"))
+                tile = T[k + "b"][:, 512 * lo:512 * hi]
+                if eng is v:
+                    for i in range(lo, hi):
+                        wait(loaded[k, i], 16)
+                    v.quantize_mx(T[k + "q"][:, 128 * lo:128 * hi], T[k + "s"][:, 128 * lo:128 * hi],
+                                  tile).then_inc(S[packed[k, lo]], 1)
+                else:
+                    eng.dma_start(tile, T[k][:, 512 * lo:512 * hi]).then_inc(S[loaded[k, lo]], 16)
+            elif k in "nl" and eng is not v:
+                j = 16 * int(step[1])
+                dst, src = (T.sn32, T.sn) if k == "n" else (T.so32, T.so)
+                eng.dma_start(dst[j:j + 16, :], src[:]).then_inc(S["ld" + k], 16)
+            elif k == "?":
+                wait("issued")
+                wait("sent0", nsent[0])
+            elif k == "y":
+                lo, hi = int(step[1]), int(step[2])
+                for m in range(lo, hi):
+                    wait("yc%d" % m)
+                eng.dma_start(T.y[:, EC * lo:EC * hi], T.yb[:, EC * lo:EC * hi]).then_inc(S.ydone, 16)
+            elif k == "z":
                 v.memset(T.zb[:], 0.0).then_inc(S.zfill, 1)
-                v.wait_ge(S.zfill, 1)
+                wait("zfill")
                 v.quantize_mx(T.landq[:, 0:Z], T.lands[:, 0:Z], T.zb[:]).then_inc(S.zquant, 1)
-                continue
-            if k == "n":
-                v.wait_ge(S.ldsn, 32)
+            elif k == "n":
+                wait("ldn", 32)
                 for j in range(4):
-                    v.tensor_copy(T.snl[32 * j:32 * j + 32, 0:4 * LC], T.sn32[0:32, :]).then_inc(S.snA, 1)
-                continue
-            if k == "N":
-                for j in range(4):
-                    v.tensor_copy(T.snl[32 * j:32 * j + 32, 4 * LC:7 * LC], T.sn32[0:32, LC:4 * LC]).then_inc(S.snB, 1)
-                continue
-            if k == "l":
-                v.wait_ge(S.ldso, 32)
+                    v.tensor_copy(T.snl[32 * j:32 * j + 32, 0:N * LC], T.sn32[0:32, :]).then_inc(S.snA, 1)
+            elif k == "N":
+                for j in range(4 if shifted else 0):
+                    v.tensor_copy(T.snl[32 * j:32 * j + 32, own:own + LC],
+                                  T.sn32[0:32, rank * LC:(rank + 1) * LC]).then_inc(S.snB, 1)
+            elif k == "l":
+                wait("ldl", 32)
                 for j in range(4):
                     v.tensor_scalar(T.sol[32 * j:32 * j + 32, :], T.so32[0:32, :], Z, None, AluOpType.add).then_inc(S.sol, 1)
-                continue
-            if k == "x":
-                v.wait_ge(S.ldx, 16)
-                v.quantize_mx(T.xq[:], T.xs[:], T.xb[:]).then_inc(S.qx, 1)
-                continue
-            if k in "apo":
-                if "x" not in seen:
-                    seen.append("x")
-                    eng.wait_ge(S.snA, 4)
-                    eng.wait_ge(S.qx, 1)
-                if k != "a" and "N" not in seen:
-                    seen.append("N")
-                    eng.wait_ge(S.snB, 4)
-                q, s, lo, hi, off = picks[k]
-                if vec:
-                    v.tensor_copy(T[q][:, lo:hi].bitcast(dt.uint32), T.xq[:, 0:TOK].bitcast(dt.uint32).indirect(off)).then_inc(S["pq" + k], 1)
+            elif k in "ABo":
+                wait("snA", 4)
+                for i in range(TOK // 128):
+                    wait(packed["x", i])
+                if k == "o" and shifted:
+                    wait("snB", 4)
+                q, s, lo, c0, c1 = picks[k]
+                hi, off = lo + 16 * (c1 - c0), T.snl[:, c0:c1]
+                if step[1] == "q":
+                    pick(T[q][:, lo:hi].bitcast(dt.uint32), T.xq[:, 0:TOK].bitcast(dt.uint32), off, step)
                 else:
-                    a.activation(T[s][:, lo:hi], T.xs[:, 0:TOK].indirect(off), ACT.Copy).then_inc(S["ps" + k], 1)
-                continue
-            m = int(step[1])
-            lo, hi = EC * m, EC * m + EC
-            if k == "w":
-                eng.wait_ge(S[ldof["w", m]], 16)
-                v.quantize_mx(T.wq[:, 512 * m:512 * m + 512], T.ws[:, 512 * m:512 * m + 512],
-                              T.wb[:, 2048 * m:2048 * m + 2048]).then_inc(S["qw%d" % m], 1)
-            elif k == "v":
-                hi = EC * int(step[2])
-                for sm in sorted({ldof["v", j] for j in range(m, int(step[2]))}):
-                    eng.wait_ge(S[sm], 16)
-                v.quantize_mx(T.vq[:, lo:hi], T.vs[:, lo:hi], T.vb[:, 4 * lo:4 * hi]).then_inc(S["qv%d" % m], 1)
+                    pick(T[s][:, lo:hi], T.xs[:, 0:TOK], off, step)
             elif k in "PS":
-                if "w" not in seen:
-                    seen.append("w")
-                    eng.wait_ge(S.zquant, 1)
-                    eng.wait_ge(S.sol, 4)
-                    eng.wait_ge(S.pqo if vec else S.pso, 1)
-                    eng.wait_ge(S.arrq if vec else S.arrs, arrive)
-                off = T.sol[:, EC // 16 * m:EC // 16 * (m + 1)]
-                if vec:
-                    v.tensor_copy(T.tokq[:, lo:hi].bitcast(dt.uint32),
-                                  T.landq[:, 0:Z + 4 * CAPP].bitcast(dt.uint32).indirect(off)).then_inc(S["tok%d" % m], 1)
+                lo, hi = EC * int(step[1]), EC * int(step[2])
+                wait("zquant")
+                wait("sol", 4)
+                wait("oq" if k == "P" else "os")
+                wait("arrq" if k == "P" else "arrs", arrive)
+                off = T.sol[:, lo // 16:hi // 16]
+                if k == "P":
+                    pick(T.tokq[:, lo:hi].bitcast(dt.uint32), T.landq[:, 0:Z + N * CAPP].bitcast(dt.uint32), off, step[:2])
                 else:
-                    a.activation(T.toks[:, lo:hi], T.lands[:, 0:Z + 4 * CAPP].indirect(off), ACT.Copy).then_inc(S["tok%d" % m], 1)
-            elif k == "R":
-                b = int(step[2])
-                out, src, done = T.h[:, 4 * lo + b:4 * hi:4], bank(("W", m, b)), S["relu%d%d" % (m, b)]
-                eng.wait_ge(S["mm%d%d" % (m, b)], 1)
-                if vec:
-                    v.tensor_scalar(out, src, 0.0, 0.05, AluOpType.max, AluOpType.mult).then_inc(done, 1)
-                else:
-                    a.activation(out, src, ACT.Relu, scale=0.05).then_inc(done, 1)
-            elif k == "Q":
-                for b in range(4):
-                    eng.wait_ge(S["relu%d%d" % (m, b)], 1)
-                v.quantize_mx(T.hq[:, lo:hi], T.hs[:, lo:hi], T.h[:, 4 * lo:4 * hi]).then_inc(S["qh%d" % m], 1)
-            elif k == "Y":
-                eng.wait_ge(S["vv%d" % m], 1)
-                if vec:
-                    v.tensor_copy(T.yb[:, lo:hi], bank(("V", m, 0))).then_inc(S["yc%d" % m], 1)
-                else:
-                    a.activation(T.yb[:, lo:hi], bank(("V", m, 0)), ACT.Copy).then_inc(S["yc%d" % m], 1)
+                    pick(T.toks[:, lo:hi], T.lands[:, 0:Z + N * CAPP], off, step[:2])
+            else:
+                m = int(step[1])
+                lo, hi = EC * m, EC * m + EC
+                if k == "R":
+                    b = int(step[2])
+                    out, src, done = T.h[:, 4 * lo + b:4 * hi:4], bank(("W", m, b)), S["relu%d%d" % (m, b)]
+                    wait("mm%d%d" % (m, b))
+                    if eng is v:
+                        v.tensor_scalar(out, src, 0.0, 0.05, AluOpType.max, AluOpType.mult).then_inc(done, 1)
+                    else:
+                        a.activation(out, src, ACT.Relu, scale=0.05).then_inc(done, 1)
+                elif k == "Q":
+                    for b in range(4):
+                        wait("relu%d%d" % (m, b))
+                    v.quantize_mx(T.hq[:, lo:hi], T.hs[:, lo:hi], T.h[:, 4 * lo:4 * hi]).then_inc(S["qh%d" % m], 1)
+                elif k == "Y":
+                    wait("vv%d" % m)
+                    if eng is v:
+                        v.tensor_copy(T.yb[:, lo:hi], bank(("V", m, 0))).then_inc(S["yc%d" % m], 1)
+                    else:
+                        a.activation(T.yb[:, lo:hi], bank(("V", m, 0)), ACT.Copy).then_inc(S["yc%d" % m], 1)
+                elif k == "W":
+                    wait(picked["S", m])
+                    wait(picked["P", m])
+                    for b in range(4):
+                        c = 512 * m + 128 * b
+                        wait(packed["w", 4 * m + b])
+                        wait(plan["W", m, b][1])
+                        t.matmul_mx(bank(("W", m, b)), T.wq[:, c:c + 128], T.ws[:, c:c + 128], T.tokq[:, lo:hi],
+                                    T.toks[:, lo:hi], True, True).then_inc(S["mm%d%d" % (m, b)], 1)
+                elif k == "V":
+                    wait(packed["v", m])
+                    wait("qh%d" % m)
+                    wait(plan["V", m, 0][1])
+                    t.matmul_mx(bank(("V", m, 0)), T.vq[:, lo:hi], T.vs[:, lo:hi], T.hq[:, lo:hi], T.hs[:, lo:hi],
+                                True, True).then_inc(S["vv%d" % m], 1)
 
     work(v, VECTOR)
     work(a, SCALAR)
-
-    t = g.tensor
-    seen = []
-    for step in tk(TENSOR):
-        m = int(step[1])
-        lo, hi = EC * m, EC * m + EC
-        if step[0] == "W":
-            t.wait_ge(S["qw%d" % m], 1)
-            t.wait_ge(S["tok%d" % m], 2)
-            for b in range(4):
-                c = 512 * m + 128 * b
-                if plan[("W", m, b)][1]:
-                    t.wait_ge(S[plan[("W", m, b)][1]], 1)
-                t.matmul_mx(bank(("W", m, b)), T.wq[:, c:c + 128], T.ws[:, c:c + 128], T.tokq[:, lo:hi], T.toks[:, lo:hi],
-                            True, True).then_inc(S["mm%d%d" % (m, b)], 1)
-        else:
-            if qvof[m] not in seen:
-                seen.append(qvof[m])
-                t.wait_ge(S[qvof[m]], 1)
-            t.wait_ge(S["qh%d" % m], 1)
-            if plan[("V", m, 0)][1]:
-                t.wait_ge(S[plan[("V", m, 0)][1]], 1)
-            t.matmul_mx(bank(("V", m, 0)), T.vq[:, lo:lo + 128], T.vs[:, lo:lo + 128], T.hq[:, lo:hi], T.hs[:, lo:hi],
-                        True, True).then_inc(S["vv%d" % m], 1)
-
-    k = 0
-    for s in tk(STORES):
-        lo, hi = int(s[0]), int(s[1])
-        for m in range(lo, hi):
-            y.wait_ge(S["yc%d" % m], 1)
-        y.dma_start(T.y[:, EC * lo:EC * hi], T.yb[:, EC * lo:EC * hi]).then_inc(S.ydone, 16)
-        k += 16
-    y.wait_ge(S.ydone, k)
+    work(t, TENSOR)
+    work(y, SYNC)
+    y.wait_ge(S.ydone, 16 * len(stores))

@@ -4,15 +4,15 @@ from concourse.mybir import AluOpType, ActivationFunctionType, dt
 CAPP, TOK, EXP, EC = 112, 384, 4, 128
 Z = 128
 LC = CAPP // 16
+U = 32
 F8 = "float8_e4m3fn_x4"
 
-SYNC = "n1 x0-2 x2-3 w0-8 w8-12 ? w12-16 v0-2 v2-4 y02 y23 y34"
-SENDS = "sAB qAB"
-VECTOR = ("z n x0-2 x2-3 As Aq Bq N oq l w0-4 w4-8 w8-12 P01 P12 P24 R03 w12-16 R13 Q0 v0-1 v1-2 R23 Q1 R31 R33 Q2 v2-3 v3-4 "
-          "Q3 Y3")
-SCALAR = "n0 l0 l1 Bs os S01 S12 S24 R00 R01 R02 R10 R11 R12 R20 R21 R22 R30 R32 Y0 Y1 Y2"
+SYNC = "n1 x0-8 x8-12 w0-32 w32-44 ? w44-56 w56-64 v0-8 v8-12 v12-16 y02 y23 y34"
+SENDS = "sA sB qAB sC qC"
+VECTOR = ("z n x0-8 x8-12 As Aq aq Bq Cq oq l w0-16 w16-32 w32-44 "
+          "P01 P12 P24 R01 w44-56 R10 w56-64 Q02 v0-8 v8-12 R33 Q23 v12-16 Q34 Y3")
+SCALAR = "n0 l0 l1 as Bs Cs os S01 S12 S24 R00 R02 R03 R11 R12 R13 R20 R21 R22 R23 R30 R31 R32 Y0 Y1 Y2"
 TENSOR = "W0 W1 W2 W3 V0 V1 V2 V3"
-PEER = 4
 
 
 def spans(order, kinds):
@@ -26,12 +26,12 @@ SCRATCH = {
     "zb": ("sbuf", [128, 4 * Z], "bfloat16"),
     "sn32": ("sbuf", [128, 4 * LC], "int32"),
     "so32": ("sbuf", [128, EXP * EC // 16], "int32"),
-    "snl": ("sbuf", [128, 40], "uint16"),
+    "snl": ("sbuf", [128, 4, LC + 1], "uint16"),
     "sol": ("sbuf", [128, EXP * EC // 16], "uint16"),
     "xq": ("sbuf", [128, TOK], F8), "xs": ("sbuf", [128, TOK], "uint8"),
     "wq": ("sbuf", [128, 512 * EXP], F8), "ws": ("sbuf", [128, 512 * EXP], "uint8"),
     "vq": ("sbuf", [128, 128 * EXP], F8), "vs": ("sbuf", [128, 128 * EXP], "uint8"),
-    "slotq": ("sbuf", [128, 4 * CAPP], F8), "slots": ("sbuf", [128, 4 * CAPP], "uint8"),
+    "slotq": ("sbuf", [128, 3 * CAPP], F8), "slots": ("sbuf", [128, 3 * CAPP], "uint8"),
     "landq": ("sbuf", [128, Z + 4 * CAPP], F8), "lands": ("sbuf", [128, Z + 4 * CAPP], "uint8"),
     "tokq": ("sbuf", [128, EXP * EC], F8), "toks": ("sbuf", [128, EXP * EC], "uint8"),
     "h": ("sbuf", [128, 4 * EXP * EC], "bfloat16"),
@@ -39,27 +39,25 @@ SCRATCH = {
     "yb": ("sbuf", [128, EXP * EC], "float32"),
     "ps": ("psum", [128, 4096], "float32"),
 }
-SEMAPHORES = (["ldn", "ldl", "zfill", "zquant", "snA", "snB", "sol", "Aq", "As", "Bq", "Bs", "oq", "os",
-               "arrq", "arrs", "ydone", "issued"]
-              + ["sent%d" % i for i in range(len(SENDS.split()))]
+SEMAPHORES = (["ldn", "ldl", "zfill", "zquant", "snl", "sol", "arrq", "arrs", "ydone", "issued", "sent"]
+              + [k + c for k in "AaBCo" for c in "qs"]
               + ["ld%s%d" % s[:2] for s in spans(SYNC + " " + SCALAR, "xwv")]
               + ["q%s%d" % s[:2] for s in spans(VECTOR, "xwv")]
-              + [k + "%d" % m for k in ("P", "S", "qh", "vv", "yc") for m in range(EXP)]
+              + [k + "%d" % m for k in ("P", "S", "Q", "vv", "yc") for m in range(EXP)]
               + [k + "%d%d" % (m, b) for k in ("mm", "relu") for m in range(EXP) for b in range(4)])
 
 
 def routes(src, cores, topo):
     away = [d for d, c in enumerate(cores) if topo.chip(c) != topo.chip(src)]
+    away.sort(key=lambda d: topo.die(cores[d]) == topo.die(src))
     peer = [d for d, c in enumerate(cores) if topo.chip(c) == topo.chip(src) and c != src]
-    out, used = {"A": [], "B": []}, []
+    out, used = {}, []
     for i, d in enumerate(away):
-        es = topo.engines(src, cores[d])
-        k = len(es) // len(away)
-        out["A"].append((d, es[i * k:(i + 1) * k]))
-        used += es[i * k:(i + 1) * k]
+        es = topo.engines(src, cores[d])[i::len(away)]
+        out["AB"[i]] = (d, es)
+        used += es
     for d in peer:
-        es = [e for e in topo.engines(src, cores[d]) if e not in used]
-        out["B"].append((d, es[::len(es) // PEER]))
+        out["C"] = (d, [e for e in topo.engines(src, cores[d]) if e not in used])
     return out
 
 
@@ -85,41 +83,38 @@ def rank_program(g, core, T, topo):
     N = len(cores)
     ACT = ActivationFunctionType
     dests = routes(core, cores, topo)
-    arrive = sum(len(es) for c in cores if c != core
-                 for part in routes(c, cores, topo).values() for d, es in part if d == rank)
+    arrive = sum(len(es) for c in cores if c != core for d, es in routes(c, cores, topo).values() if d == rank)
     v, a, y, t = g.vector, g.scalar, g.sync, g.tensor
 
     loaded = {(k, i): "ld%s%d" % (k, lo) for k, lo, hi in spans(SYNC + " " + SCALAR, "xwv") for i in range(lo, hi)}
     packed = {(k, i): "q%s%d" % (k, lo) for k, lo, hi in spans(VECTOR, "xwv") for i in range(lo, hi)}
-    picked = {(s[0], m): s[:2] for s in (VECTOR + " " + SCALAR).split() if s[0] in "PS" for m in range(int(s[1]), int(s[2]))}
+    picked = {(s[0], m): s[:2] for s in (VECTOR + " " + SCALAR).split() if s[0] in "PSQ" for m in range(int(s[1]), int(s[2]))}
     stores = [s for s in (SYNC + " " + SCALAR).split() if s[0] == "y"]
 
-    shifted = rank * LC % 2 == 1
-    own = N * LC if shifted else rank * LC
-    picks = {"o": ("landq", "lands", Z + rank * CAPP, own, own + LC)}
-    for k in "AB":
-        c0, c1 = dests[k][0][0] * LC // 2 * 2, (dests[k][-1][0] + 1) * LC
-        picks[k] = ("slotq", "slots", 16 * c0, c0, c1)
+    picks = {"o": ("landq", "lands", Z + rank * CAPP, rank, 0, LC)}
+    for i, k in enumerate("ABC"):
+        picks[k] = ("slotq", "slots", i * CAPP, dests[k][0], 0, LC)
+    picks["A"], picks["a"] = picks["A"][:4] + (0, 4), picks["A"][:4] + (4, LC)
 
-    nsent = []
+    nsent = 0
     for s in SENDS.split():
         trs = []
         for k in s[1:]:
-            g.wait_ge(S[k + s[0]], 1)
-            for d, es in dests[k]:
-                rid, pid, _ = topo.addr(cores[d])
-                c0, l0 = d * CAPP, Z + rank * CAPP
-                if s[0] == "q":
-                    src, dst = T.slotq[:, c0:c0 + CAPP].bitcast(dt.uint8), T.landq[:, l0:l0 + CAPP].bitcast(dt.uint8)
-                else:
-                    src, dst = T.slots[:, c0:c0 + CAPP], T.lands[:, l0:l0 + CAPP]
-                trs.append(RemoteDMATransfer(dst_ids=[DstId(rid=rid, pnc=pid)], dma_engine_mask=sum(1 << e for e in es),
-                                             remote_sem=S["arr" + s[0]], src=src, dst=dst))
-        g.remote_dma_fused(trs, local_sem=S["sent%d" % len(nsent)])
-        nsent.append(sum(len(es) for k in s[1:] for _, es in dests[k]))
+            for part in ("Aa" if k == "A" else k):
+                g.wait_ge(S[part + s[0]], 1)
+            d, es = dests[k]
+            rid, pid, _ = topo.addr(cores[d])
+            c0, l0 = picks[k][2], Z + rank * CAPP
+            if s[0] == "q":
+                src, dst = T.slotq[:, c0:c0 + CAPP].bitcast(dt.uint8), T.landq[:, l0:l0 + CAPP].bitcast(dt.uint8)
+            else:
+                src, dst = T.slots[:, c0:c0 + CAPP], T.lands[:, l0:l0 + CAPP]
+            trs.append(RemoteDMATransfer(dst_ids=[DstId(rid=rid, pnc=pid)], dma_engine_mask=sum(1 << e for e in es),
+                                         remote_sem=S["arr" + s[0]], src=src, dst=dst))
+            nsent += len(es)
+        g.remote_dma_fused(trs, local_sem=S.sent)
     g.sem_inc(S.issued, 1)
-    for i, n in enumerate(nsent):
-        g.wait_ge(S["sent%d" % i], n)
+    g.wait_ge(S.sent, nsent)
 
     plan = banks()
 
@@ -134,6 +129,10 @@ def rank_program(g, core, T, topo):
                 seen.append(name)
                 eng.wait_ge(S[name], n)
 
+        def wait_packed(k, lo, hi):
+            for i in range(lo // U, hi // U):
+                wait(packed[k, i])
+
         def pick(out, win, off, done):
             if eng is v:
                 v.tensor_copy(out, win.indirect(off)).then_inc(S[done], 1)
@@ -144,21 +143,20 @@ def rank_program(g, core, T, topo):
             k = step[0]
             if k in "xwv":
                 lo, hi = (int(n) for n in step[1:].split("-"))
-                tile = T[k + "b"][:, 512 * lo:512 * hi]
+                tile = T[k + "b"][:, 4 * U * lo:4 * U * hi]
                 if eng is v:
                     for i in range(lo, hi):
                         wait(loaded[k, i], 16)
-                    v.quantize_mx(T[k + "q"][:, 128 * lo:128 * hi], T[k + "s"][:, 128 * lo:128 * hi],
+                    v.quantize_mx(T[k + "q"][:, U * lo:U * hi], T[k + "s"][:, U * lo:U * hi],
                                   tile).then_inc(S[packed[k, lo]], 1)
                 else:
-                    eng.dma_start(tile, T[k][:, 512 * lo:512 * hi]).then_inc(S[loaded[k, lo]], 16)
+                    eng.dma_start(tile, T[k][:, 4 * U * lo:4 * U * hi]).then_inc(S[loaded[k, lo]], 16)
             elif k in "nl" and eng is not v:
                 j = 16 * int(step[1])
                 dst, src = (T.sn32, T.sn) if k == "n" else (T.so32, T.so)
                 eng.dma_start(dst[j:j + 16, :], src[:]).then_inc(S["ld" + k], 16)
             elif k == "?":
                 wait("issued")
-                wait("sent0", nsent[0])
             elif k == "y":
                 lo, hi = int(step[1]), int(step[2])
                 for m in range(lo, hi):
@@ -171,23 +169,16 @@ def rank_program(g, core, T, topo):
             elif k == "n":
                 wait("ldn", 32)
                 for j in range(4):
-                    v.tensor_copy(T.snl[32 * j:32 * j + 32, 0:N * LC], T.sn32[0:32, :]).then_inc(S.snA, 1)
-            elif k == "N":
-                for j in range(4 if shifted else 0):
-                    v.tensor_copy(T.snl[32 * j:32 * j + 32, own:own + LC],
-                                  T.sn32[0:32, rank * LC:(rank + 1) * LC]).then_inc(S.snB, 1)
+                    v.tensor_copy(T.snl[32 * j:32 * j + 32, :, 0:LC], T.sn32[0:32, :]).then_inc(S.snl, 1)
             elif k == "l":
                 wait("ldl", 32)
                 for j in range(4):
                     v.tensor_scalar(T.sol[32 * j:32 * j + 32, :], T.so32[0:32, :], Z, None, AluOpType.add).then_inc(S.sol, 1)
-            elif k in "ABo":
-                wait("snA", 4)
-                for i in range(TOK // 128):
-                    wait(packed["x", i])
-                if k == "o" and shifted:
-                    wait("snB", 4)
-                q, s, lo, c0, c1 = picks[k]
-                hi, off = lo + 16 * (c1 - c0), T.snl[:, c0:c1]
+            elif k in "AaBCo":
+                wait("snl", 4)
+                wait_packed("x", 0, TOK)
+                q, s, lo, d, c0, c1 = picks[k]
+                lo, hi, off = lo + 16 * c0, lo + 16 * c1, T.snl[:, d, c0:c1]
                 if step[1] == "q":
                     pick(T[q][:, lo:hi].bitcast(dt.uint32), T.xq[:, 0:TOK].bitcast(dt.uint32), off, step)
                 else:
@@ -215,9 +206,11 @@ def rank_program(g, core, T, topo):
                     else:
                         a.activation(out, src, ACT.Relu, scale=0.05).then_inc(done, 1)
                 elif k == "Q":
-                    for b in range(4):
-                        wait("relu%d%d" % (m, b))
-                    v.quantize_mx(T.hq[:, lo:hi], T.hs[:, lo:hi], T.h[:, 4 * lo:4 * hi]).then_inc(S["qh%d" % m], 1)
+                    hi = EC * int(step[2])
+                    for i in range(m, int(step[2])):
+                        for b in range(4):
+                            wait("relu%d%d" % (i, b))
+                    v.quantize_mx(T.hq[:, lo:hi], T.hs[:, lo:hi], T.h[:, 4 * lo:4 * hi]).then_inc(S[step[:2]], 1)
                 elif k == "Y":
                     wait("vv%d" % m)
                     if eng is v:
@@ -229,13 +222,13 @@ def rank_program(g, core, T, topo):
                     wait(picked["P", m])
                     for b in range(4):
                         c = 512 * m + 128 * b
-                        wait(packed["w", 4 * m + b])
+                        wait_packed("w", c, c + 128)
                         wait(plan["W", m, b][1])
                         t.matmul_mx(bank(("W", m, b)), T.wq[:, c:c + 128], T.ws[:, c:c + 128], T.tokq[:, lo:hi],
                                     T.toks[:, lo:hi], True, True).then_inc(S["mm%d%d" % (m, b)], 1)
                 elif k == "V":
-                    wait(packed["v", m])
-                    wait("qh%d" % m)
+                    wait_packed("v", lo, hi)
+                    wait(picked["Q", m])
                     wait(plan["V", m, 0][1])
                     t.matmul_mx(bank(("V", m, 0)), T.vq[:, lo:hi], T.vs[:, lo:hi], T.hq[:, lo:hi], T.hs[:, lo:hi],
                                 True, True).then_inc(S["vv%d" % m], 1)

from concourse.bass import DstId, RemoteDMATransfer
from concourse.mybir import AluOpType, ActivationFunctionType, dt

CAPP, TOK, EXP, EC = 112, 384, 4, 128
Z = 128
LC = CAPP // 16
U = 32
F8 = "float8_e4m3fn_x4"

SYNC = "n1 x0-8 x8-12 w0-32 w32-44 ? w44-56 w56-64 v0-8 v8-12 v12-16 y02 y23 y34"
SENDS = "sA sB qAB sC qC"
VECTOR = ("z n x0-8 x8-12 As Aq aq Bq Cq oq l w0-16 w16-32 w32-44 "
          "P01 P12 P24 R01 w44-56 R10 w56-64 Q02 v0-8 v8-12 R33 Q23 v12-16 Q34 Y3")
SCALAR = "n0 l0 l1 as Bs Cs os S01 S12 S24 R00 R02 R03 R11 R12 R13 R20 R21 R22 R23 R30 R31 R32 Y0 Y1 Y2"
TENSOR = "W0 W1 W2 W3 V0 V1 V2 V3"


def spans(order, kinds):
    return [(s[0],) + tuple(int(n) for n in s[1:].split("-")) for s in order.split() if s[0] in kinds and "-" in s]


SCRATCH = {
    "xb": ("sbuf", [128, 4 * TOK], "bfloat16"),
    "wb": ("sbuf", [128, 2048 * EXP], "bfloat16"),
    "vb": ("sbuf", [128, 512 * EXP], "bfloat16"),
    "zb": ("sbuf", [128, 4 * Z], "bfloat16"),
    "sn32": ("sbuf", [128, 4 * LC], "int32"),
    "so32": ("sbuf", [128, EXP * EC // 16], "int32"),
    "snl": ("sbuf", [128, 4, LC + 1], "uint16"),
    "sol": ("sbuf", [128, EXP * EC // 16], "uint16"),
    "xq": ("sbuf", [128, TOK], F8), "xs": ("sbuf", [128, TOK], "uint8"),
    "wq": ("sbuf", [128, 512 * EXP], F8), "ws": ("sbuf", [128, 512 * EXP], "uint8"),
    "vq": ("sbuf", [128, 128 * EXP], F8), "vs": ("sbuf", [128, 128 * EXP], "uint8"),
    "slotq": ("sbuf", [128, 3 * CAPP], F8), "slots": ("sbuf", [128, 3 * CAPP], "uint8"),
    "landq": ("sbuf", [128, Z + 4 * CAPP], F8), "lands": ("sbuf", [128, Z + 4 * CAPP], "uint8"),
    "tokq": ("sbuf", [128, EXP * EC], F8), "toks": ("sbuf", [128, EXP * EC], "uint8"),
    "h": ("sbuf", [128, 4 * EXP * EC], "bfloat16"),
    "hq": ("sbuf", [128, EXP * EC], F8), "hs": ("sbuf", [128, EXP * EC], "uint8"),
    "yb": ("sbuf", [128, EXP * EC], "float32"),
    "ps": ("psum", [128, 4096], "float32"),
}
SEMAPHORES = (["ldn", "ldl", "zfill", "zquant", "snl", "sol", "arrq", "arrs", "ydone", "issued", "sent"]
              + [k + c for k in "AaBCo" for c in "qs"]
              + ["ld%s%d" % s[:2] for s in spans(SYNC + " " + SCALAR, "xwv")]
              + ["q%s%d" % s[:2] for s in spans(VECTOR, "xwv")]
              + [k + "%d" % m for k in ("P", "S", "Q", "vv", "yc") for m in range(EXP)]
              + [k + "%d%d" % (m, b) for k in ("mm", "relu") for m in range(EXP) for b in range(4)])


def routes(src, cores, topo):
    away = [d for d, c in enumerate(cores) if topo.chip(c) != topo.chip(src)]
    away.sort(key=lambda d: topo.die(cores[d]) == topo.die(src))
    peer = [d for d, c in enumerate(cores) if topo.chip(c) == topo.chip(src) and c != src]
    out, used = {}, []
    for i, d in enumerate(away):
        es = topo.engines(src, cores[d])[i::len(away)]
        out["AB"[i]] = (d, es)
        used += es
    for d in peer:
        out["C"] = (d, [e for e in topo.engines(src, cores[d]) if e not in used])
    return out


def banks():
    plan, held, i = {}, [None] * 8, 0
    for t in TENSOR.split():
        m = int(t[1])
        for p in ([("W", m, b) for b in range(4)] if t[0] == "W" else [("V", m, 0)]):
            k = i % 8
            o = held[k]
            plan[p] = (k, None if o is None else "relu%d%d" % o[1:] if o[0] == "W" else "yc%d" % o[1])
            held[k] = p
            i += 1
    return plan


def rank_program(g, core, T, topo):
    rank = T.rank_of(core)
    if rank is None:
        return
    S = T.sem
    cores = list(T.cores)
    N = len(cores)
    ACT = ActivationFunctionType
    dests = routes(core, cores, topo)
    arrive = sum(len(es) for c in cores if c != core for d, es in routes(c, cores, topo).values() if d == rank)
    v, a, y, t = g.vector, g.scalar, g.sync, g.tensor

    loaded = {(k, i): "ld%s%d" % (k, lo) for k, lo, hi in spans(SYNC + " " + SCALAR, "xwv") for i in range(lo, hi)}
    packed = {(k, i): "q%s%d" % (k, lo) for k, lo, hi in spans(VECTOR, "xwv") for i in range(lo, hi)}
    picked = {(s[0], m): s[:2] for s in (VECTOR + " " + SCALAR).split() if s[0] in "PSQ" for m in range(int(s[1]), int(s[2]))}
    stores = [s for s in (SYNC + " " + SCALAR).split() if s[0] == "y"]

    picks = {"o": ("landq", "lands", Z + rank * CAPP, rank, 0, LC)}
    for i, k in enumerate("ABC"):
        picks[k] = ("slotq", "slots", i * CAPP, dests[k][0], 0, LC)
    picks["A"], picks["a"] = picks["A"][:4] + (0, 4), picks["A"][:4] + (4, LC)

    nsent = 0
    for s in SENDS.split():
        trs = []
        for k in s[1:]:
            for part in ("Aa" if k == "A" else k):
                g.wait_ge(S[part + s[0]], 1)
            d, es = dests[k]
            rid, pid, _ = topo.addr(cores[d])
            c0, l0 = picks[k][2], Z + rank * CAPP
            if s[0] == "q":
                src, dst = T.slotq[:, c0:c0 + CAPP].bitcast(dt.uint8), T.landq[:, l0:l0 + CAPP].bitcast(dt.uint8)
            else:
                src, dst = T.slots[:, c0:c0 + CAPP], T.lands[:, l0:l0 + CAPP]
            trs.append(RemoteDMATransfer(dst_ids=[DstId(rid=rid, pnc=pid)], dma_engine_mask=sum(1 << e for e in es),
                                         remote_sem=S["arr" + s[0]], src=src, dst=dst))
            nsent += len(es)
        g.remote_dma_fused(trs, local_sem=S.sent)
    g.sem_inc(S.issued, 1)
    g.wait_ge(S.sent, nsent)

    plan = banks()

    def bank(p):
        return T.ps[:, 512 * plan[p][0]:512 * plan[p][0] + EC]

    def work(eng, order):
        seen = []

        def wait(name, n=1):
            if name and name not in seen:
                seen.append(name)
                eng.wait_ge(S[name], n)

        def wait_packed(k, lo, hi):
            for i in range(lo // U, hi // U):
                wait(packed[k, i])

        def pick(out, win, off, done):
            if eng is v:
                v.tensor_copy(out, win.indirect(off)).then_inc(S[done], 1)
            else:
                a.activation(out, win.indirect(off), ACT.Copy).then_inc(S[done], 1)

        for step in order.split():
            k = step[0]
            if k in "xwv":
                lo, hi = (int(n) for n in step[1:].split("-"))
                tile = T[k + "b"][:, 4 * U * lo:4 * U * hi]
                if eng is v:
                    for i in range(lo, hi):
                        wait(loaded[k, i], 16)
                    v.quantize_mx(T[k + "q"][:, U * lo:U * hi], T[k + "s"][:, U * lo:U * hi],
                                  tile).then_inc(S[packed[k, lo]], 1)
                else:
                    eng.dma_start(tile, T[k][:, 4 * U * lo:4 * U * hi]).then_inc(S[loaded[k, lo]], 16)
            elif k in "nl" and eng is not v:
                j = 16 * int(step[1])
                dst, src = (T.sn32, T.sn) if k == "n" else (T.so32, T.so)
                eng.dma_start(dst[j:j + 16, :], src[:]).then_inc(S["ld" + k], 16)
            elif k == "?":
                wait("issued")
            elif k == "y":
                lo, hi = int(step[1]), int(step[2])
                for m in range(lo, hi):
                    wait("yc%d" % m)
                eng.dma_start(T.y[:, EC * lo:EC * hi], T.yb[:, EC * lo:EC * hi]).then_inc(S.ydone, 16)
            elif k == "z":
                v.memset(T.zb[:], 0.0).then_inc(S.zfill, 1)
                wait("zfill")
                v.quantize_mx(T.landq[:, 0:Z], T.lands[:, 0:Z], T.zb[:]).then_inc(S.zquant, 1)
            elif k == "n":
                wait("ldn", 32)
                for j in range(4):
                    v.tensor_copy(T.snl[32 * j:32 * j + 32, :, 0:LC], T.sn32[0:32, :]).then_inc(S.snl, 1)
            elif k == "l":
                wait("ldl", 32)
                for j in range(4):
                    v.tensor_scalar(T.sol[32 * j:32 * j + 32, :], T.so32[0:32, :], Z, None, AluOpType.add).then_inc(S.sol, 1)
            elif k in "AaBCo":
                wait("snl", 4)
                wait_packed("x", 0, TOK)
                q, s, lo, d, c0, c1 = picks[k]
                lo, hi, off = lo + 16 * c0, lo + 16 * c1, T.snl[:, d, c0:c1]
                if step[1] == "q":
                    pick(T[q][:, lo:hi].bitcast(dt.uint32), T.xq[:, 0:TOK].bitcast(dt.uint32), off, step)
                else:
                    pick(T[s][:, lo:hi], T.xs[:, 0:TOK], off, step)
            elif k in "PS":
                lo, hi = EC * int(step[1]), EC * int(step[2])
                wait("zquant")
                wait("sol", 4)
                wait("oq" if k == "P" else "os")
                wait("arrq" if k == "P" else "arrs", arrive)
                off = T.sol[:, lo // 16:hi // 16]
                if k == "P":
                    pick(T.tokq[:, lo:hi].bitcast(dt.uint32), T.landq[:, 0:Z + N * CAPP].bitcast(dt.uint32), off, step[:2])
                else:
                    pick(T.toks[:, lo:hi], T.lands[:, 0:Z + N * CAPP], off, step[:2])
            else:
                m = int(step[1])
                lo, hi = EC * m, EC * m + EC
                if k == "R":
                    b = int(step[2])
                    out, src, done = T.h[:, 4 * lo + b:4 * hi:4], bank(("W", m, b)), S["relu%d%d" % (m, b)]
                    wait("mm%d%d" % (m, b))
                    if eng is v:
                        v.tensor_scalar(out, src, 0.0, 0.05, AluOpType.max, AluOpType.mult).then_inc(done, 1)
                    else:
                        a.activation(out, src, ACT.Relu, scale=0.05).then_inc(done, 1)
                elif k == "Q":
                    hi = EC * int(step[2])
                    for i in range(m, int(step[2])):
                        for b in range(4):
                            wait("relu%d%d" % (i, b))
                    v.quantize_mx(T.hq[:, lo:hi], T.hs[:, lo:hi], T.h[:, 4 * lo:4 * hi]).then_inc(S[step[:2]], 1)
                elif k == "Y":
                    wait("vv%d" % m)
                    if eng is v:
                        v.tensor_copy(T.yb[:, lo:hi], bank(("V", m, 0))).then_inc(S["yc%d" % m], 1)
                    else:
                        a.activation(T.yb[:, lo:hi], bank(("V", m, 0)), ACT.Copy).then_inc(S["yc%d" % m], 1)
                elif k == "W":
                    wait(picked["S", m])
                    wait(picked["P", m])
                    for b in range(4):
                        c = 512 * m + 128 * b
                        wait_packed("w", c, c + 128)
                        wait(plan["W", m, b][1])
                        t.matmul_mx(bank(("W", m, b)), T.wq[:, c:c + 128], T.ws[:, c:c + 128], T.tokq[:, lo:hi],
                                    T.toks[:, lo:hi], True, True).then_inc(S["mm%d%d" % (m, b)], 1)
                elif k == "V":
                    wait_packed("v", lo, hi)
                    wait(picked["Q", m])
                    wait(plan["V", m, 0][1])
                    t.matmul_mx(bank(("V", m, 0)), T.vq[:, lo:hi], T.vs[:, lo:hi], T.hq[:, lo:hi], T.hs[:, lo:hi],
                                True, True).then_inc(S["vv%d" % m], 1)

    work(v, VECTOR)
    work(a, SCALAR)
    work(t, TENSOR)
    work(y, SYNC)
    y.wait_ge(S.ydone, 16 * len(stores))
